import numpy as np
import ml_dtypes


def mxq(x, axis, fmt="e4m3"):
    dtype, down = {"e4m3": (ml_dtypes.float8_e4m3fn, 7), "e5m2": (ml_dtypes.float8_e5m2, 14)}[fmt]
    v = np.moveaxis(np.asarray(x, np.float32).astype(ml_dtypes.bfloat16).astype(np.float64), axis, -1)
    blocks = v.reshape(v.shape[:-1] + (-1, 32))
    amax = np.abs(blocks).max(-1, keepdims=True)
    byte = np.maximum(np.where(amax > 0, np.frexp(amax)[1] - 1 + 127, 0) - down, 1)
    scale = np.exp2(byte - 127.0)
    codes = (blocks / scale).astype(np.float32).astype(dtype).astype(np.float64)
    return np.moveaxis((codes * scale).reshape(v.shape), -1, axis)


WIDE = False


def mx_kscale(k):
    if not WIDE:
        return np.ones(k)
    levels = np.array([10, -10, 5, -5, 0])
    if k % 512:
        return np.exp2(np.random.permutation(np.resize(levels, k // 32))).repeat(32)
    a = np.empty((k // 512, 16))
    for p in range(k // 512):
        a[p, :8] = np.random.permutation(np.resize(levels, 8))
        for g in range(8):
            far = levels[np.abs(levels - a[p, g]) >= 10]
            a[p, g + 8] = far[np.random.randint(len(far))]
    return np.exp2(a.ravel()).repeat(32)


def f64(x):
    return np.asarray(x).astype(np.float64)


def striped(idx):
    return np.tile(idx.reshape(-1, 16).T, (8, 1)).astype(np.uint16)


def unstriped(offs):
    return offs[:16].T.reshape(-1).astype(np.int64)


E2M1 = np.array([0.0, 0.5, 1.0, 1.5, 2.0, 3.0, 4.0, 6.0, -0.0, -0.5, -1.0, -1.5, -2.0, -3.0, -4.0, -6.0])


def pack_weight(w, fmt):
    k, n = w.shape
    w = f64(np.asarray(w, np.float32).astype(ml_dtypes.bfloat16)).reshape(k // 32, 32, n)
    amax = np.abs(w).max(1)
    if fmt == "e4m3":
        byte = np.frexp(amax)[1] - 1 + 127 - 7
    else:
        mant, ex = np.frexp(amax / 6.0)
        byte = np.where(mant > 0.5, ex, ex - 1) + 127
    byte = np.clip(np.where(amax > 0, byte, 1), 1, 254)
    scaled = (w * np.exp2(127.0 - byte)[:, None, :]).reshape(k, n).astype(np.float32)
    by_word = np.ascontiguousarray(scaled.reshape(k // 512, 128, 4, n).transpose(0, 1, 3, 2))
    if fmt == "e4m3":
        words = by_word.astype(ml_dtypes.float8_e4m3fn).view(np.uint8)
    else:
        c = by_word.astype(ml_dtypes.float4_e2m1fn).view(np.uint8) & 0xF
        words = (c[..., 0::2] | (c[..., 1::2] << 4)).reshape(k // 512, 128, 2 * n)
    return np.ascontiguousarray(words), np.ascontiguousarray(byte.astype(np.uint8).reshape(k // 512, 16, n))


def unpack_weight(words, scales, fmt):
    g, _, n = scales.shape
    words = np.ascontiguousarray(words).reshape(g, 128, n, -1)
    if fmt == "e4m3":
        vals = words.view(ml_dtypes.float8_e4m3fn).astype(np.float64)
    else:
        nib = np.empty((g, 128, n, 4), np.uint8)
        nib[..., 0::2] = words & 0xF
        nib[..., 1::2] = words >> 4
        vals = E2M1[nib]
    vals = vals * np.repeat(np.exp2(scales.astype(np.float64) - 127.0), 8, axis=1)[..., None]
    return vals.transpose(0, 1, 3, 2).reshape(g * 512, n)


def relu2(v):
    return np.maximum(v, 0.0) ** 2


K, T, E, C, H, N = 512, 1024, 24, 128, 512, 128
TOP = 3


def by_expert(wq, xq):
    return np.concatenate([wq[e].T @ xq[:, e * C:(e + 1) * C] for e in range(E)], axis=1)


def setup_inputs():
    n = np.random.standard_normal
    s = mx_kscale(K)[:, None]
    u = mx_kscale(H)
    deal = np.repeat(np.arange(E), C).reshape(TOP, T)[:, np.random.permutation(T)]
    deal = np.take_along_axis(deal, np.argsort(np.random.rand(TOP, T), axis=0), axis=0)
    for _ in range(8):
        s_, t_ = np.random.permutation(T).reshape(2, -1); r = np.random.randint(TOP, size=T // 2); x, y = deal[r, s_].copy(), deal[r, t_].copy()
        ok = ~((deal[:, s_] == y).any(0) | (deal[:, t_] == x).any(0)); deal[r[ok], s_[ok]] = y[ok]; deal[r[ok], t_[ok]] = x[ok]
    order = np.lexsort((np.random.rand(TOP * T), deal.reshape(-1)))
    slot_token = order % T; pos = np.empty(TOP * T, np.int64); pos[order] = np.arange(TOP * T); pos = pos.reshape(TOP, T)
    g = np.random.uniform(0.5, 1.5, (TOP, T)); g = g / g.sum(0)
    w1 = [pack_weight(m, "e2m1") for m in n((E, K, H)) / np.sqrt(K) / s[None] * u[None, None, :]]
    w2 = [pack_weight(m, "e2m1") for m in n((E, H, N)) / np.sqrt(H) / u[None, :, None] ** 2]
    return {
        "xT": (n((K, T)) * s).astype(np.float32),
        "w1_words": np.stack([m[0] for m in w1]),
        "w1_scales": np.stack([m[1] for m in w1]),
        "w2_words": np.stack([m[0] for m in w2]),
        "w2_scales": np.stack([m[1] for m in w2]),
        "gate": np.stack([np.tile(r, (N, 1)) for r in g]).astype(np.float32),
        "offs": striped(slot_token),
        "pos1": striped(pos[0]),
        "pos2": striped(pos[1]),
        "pos3": striped(pos[2]),
    }


def reference(xT, w1_words, w1_scales, w2_words, w2_scales, gate, offs, pos1, pos2, pos3):
    idx = unstriped(offs)
    w1 = np.stack([unpack_weight(w1_words[e], w1_scales[e], "e2m1") for e in range(E)])
    w2 = np.stack([unpack_weight(w2_words[e], w2_scales[e], "e2m1") for e in range(E)])
    xq = mxq(f64(xT)[:, idx], 0, "e4m3")
    h = relu2(by_expert(w1, xq))
    y = by_expert(w2, mxq(h, 0, "e4m3"))
    return sum(f64(gate[r]) * y[:, unstriped(p)] for r, p in enumerate((pos1, pos2, pos3)))

@@ -1,0 +1,229 @@
+from contextlib import ExitStack
+
+import concourse.mybir as mybir
+from concourse.masks import make_identity
+
+K, T, E, C, H, N = 512, 1024, 24, 128, 512, 128
+TOP = 3
+S = E * C
+FLOPS = 2 * S * (K * H + H * N)
+
+F32 = mybir.dt.float32
+BF16 = mybir.dt.bfloat16
+I32 = mybir.dt.int32
+U32 = mybir.dt.uint32
+U16 = mybir.dt.uint16
+U8 = mybir.dt.uint8
+FP8X4 = mybir.dt.float8_e4m3fn_x4
+FP4X4 = mybir.dt.float4_e2m1fn_x4
+ACT = mybir.ActivationFunctionType
+ALU = mybir.AluOpType
+
+P = 128
+PACK = 4
+
+X_CUTS = [0, 256, 512, 768, 896, 1024]
+X_ON_SCALAR = (0, 2)
+GATHERS = [1, 1] + [2] * 11
+RELU_ON_VECTOR = (5, 7, 9, 11, 13, 15, 17, 19, 21, 23)
+OUT_CUTS = [0, 512, 768, 1024]
+
+
+def tile_moe_tk_mlp_relu2_kernel(
+    tc, xT, w1_words, w1_scales, w2_words, w2_scales, gate, offs, pos1, pos2, pos3, out
+):
+    nc = tc.nc
+    with ExitStack() as ctx:
+        held = ctx.enter_context(tc.tile_pool(name="held", bufs=1))
+        ring = ctx.enter_context(tc.tile_pool(name="ring", bufs=4))
+        ring2 = ctx.enter_context(tc.tile_pool(name="ring2", bufs=2))
+        psum_a = ctx.enter_context(tc.psum_pool(name="psum_a", bufs=3))
+        psum_b = ctx.enter_context(tc.psum_pool(name="psum_b", bufs=3))
+        psum_y = ctx.enter_context(tc.psum_pool(name="psum_y", bufs=2))
+
+        offs_sb = held.tile([P, S // 16], U16, name="offs_sb")
+        pos_sb = [held.tile([P, T // 16], U16, name=f"pos{r}_sb") for r in range(TOP)]
+        x_words = held.tile([P, T], U32, name="x_words", align_bytes=64)
+        x_scales = held.tile([P, T], U8, name="x_scales", align_bytes=64)
+        w1 = held.tile([P, E, 2 * H], U8, name="w1", align_bytes=64)
+        w1s = held.tile([P, E, H], U8, name="w1s", align_bytes=64)
+        w2 = held.tile([P, E, 2 * N], U8, name="w2", align_bytes=64)
+        w2s = held.tile([P, E, N], U8, name="w2s", align_bytes=64)
+        gate_sb = held.tile([P, TOP, T], F32, name="gate_sb")
+        y = held.tile([P, S], F32, name="y")
+        ident = held.tile([P, P], F32, name="ident")
+
+        nc.gpsimd.memset(x_scales[:], 0)
+        make_identity(nc, ident[:])
+        nc.vector.memset(w1s[:, 0:6, :].bitcast(I32), 0)
+        nc.vector.memset(w2s[:].bitcast(I32), 0)
+        nc.vector.memset(w1s[:, 6:E, :].bitcast(I32), 0)
+
+        x_raw = []
+        x_view = xT.rearrange("(p j) t -> p j t", j=PACK)
+        for i in range(len(X_CUTS) - 1):
+            t0, t1 = X_CUTS[i], X_CUTS[i + 1]
+            raw = held.tile([P, PACK, t1 - t0], F32, name=f"x_raw{i}")
+            nc.sync.dma_start(raw[:], x_view[:, :, t0:t1])
+            x_raw.append(raw)
+            if i == len(X_CUTS) - 3:
+                nc.sync.dma_start(offs_sb[:], offs)
+
+        def load_w1(a, b):
+            nc.sync.dma_start(
+                w1[:, a:b, :].bitcast(I32), w1_words[a:b, 0].rearrange("e p n -> p e n").bitcast(I32)
+            )
+
+        def load_w2(a, b):
+            nc.sync.dma_start(
+                w2[:, a:b, :].bitcast(I32), w2_words[a:b, 0].rearrange("e p n -> p e n").bitcast(I32)
+            )
+
+        def load_scales(tile, src, a, b):
+            for q in range(4):
+                nc.sync.dma_start(
+                    tile[32 * q : 32 * q + 4, a:b, :].bitcast(I32),
+                    src[a:b, 0, 4 * q : 4 * q + 4, :].rearrange("e q n -> q e n").bitcast(I32),
+                )
+
+        load_w1(0, 2)
+        load_scales(w1s, w1_scales, 0, 6)
+        load_scales(w2s, w2_scales, 0, E)
+        load_w1(2, 5)
+        load_w2(0, 8)
+        load_scales(w1s, w1_scales, 6, E)
+        load_w1(5, 9)
+        load_w1(9, 14)
+        load_w2(8, E)
+        load_w1(14, 19)
+        load_w1(19, E)
+        for r, p in enumerate((pos1, pos2, pos3)):
+            nc.sync.dma_start(pos_sb[r][:], p)
+        nc.sync.dma_start(gate_sb[:], gate.rearrange("r p t -> p r t"))
+
+        for i in range(len(X_CUTS) - 1):
+            t0, t1 = X_CUTS[i], X_CUTS[i + 1]
+            grouped = held.tile([P, t1 - t0, PACK], BF16, name=f"x_grouped{i}", align_bytes=64)
+            src = x_raw[i][:].rearrange("p j t -> p t j")
+            if i in X_ON_SCALAR:
+                nc.scalar.activation(grouped[:], src, ACT.Copy)
+            else:
+                nc.vector.tensor_copy(grouped[:], src)
+            nc.vector.quantize_mx(
+                out=x_words[:, t0:t1].bitcast(FP8X4),
+                scales=x_scales[:, t0:t1],
+                in_=grouped[:].rearrange("p t j -> p (t j)"),
+            )
+
+        gath = ctx.enter_context(tc.tile_pool(name="gath", bufs=3))
+        gathered = {}
+
+        def gather(e0, n):
+            cols = slice(e0 * C // 16, (e0 + n) * C // 16)
+            gw = gath.tile([P, n * C], U32, name="gw", align_bytes=64)
+            gs = gath.tile([P, n * C], U8, name="gs", align_bytes=64)
+            nc.vector.tensor_copy(gw[:], x_words[:].indirect(offs_sb[:, cols]))
+            nc.vector.tensor_copy(gs[:], x_scales[:].indirect(offs_sb[:, cols]))
+            for e in range(e0, e0 + n):
+                gathered[e] = (gw, gs, (e - e0) * C)
+
+        acts = {}
+        hs = {}
+        y_bank = {}
+
+        def first(e):
+            gw, gs, c0 = gathered[e]
+            a = psum_a.tile([C, H], F32, name="a")
+            nc.tensor.matmul_mx(
+                out=a[:],
+                lhsT=gw[:, c0 : c0 + C].bitcast(FP8X4),
+                lhsT_scale=gs[:, c0 : c0 + C],
+                rhs=w1[:, e, :].bitcast(FP4X4),
+                rhs_scale=w1s[:, e, :],
+                start=True,
+                stop=True,
+            )
+            r = ring.tile([C, PACK, P], F32, name="r")
+            src = a[:].rearrange("s (m t) -> s t m", t=PACK)
+            if e in RELU_ON_VECTOR:
+                nc.vector.tensor_scalar_max(r[:], src, 0.0)
+            else:
+                nc.scalar.activation(r[:], src, ACT.Relu)
+            acts[e] = r
+
+        def turn(e):
+            b = psum_b.tile([P, PACK, C], F32, name="b")
+            for t in range(PACK):
+                nc.tensor.transpose(b[:, t, :], acts[e][:, t, :], ident[:])
+            h = ring.tile([P, C, PACK], BF16, name="h", align_bytes=64)
+            nc.scalar.activation(h[:], b[:].rearrange("p t s -> p s t"), ACT.Square)
+            hs[e] = h
+
+        def second(e):
+            hw = ring.tile([P, C], U32, name="hw", align_bytes=64)
+            hsc = ring.tile([P, C], U8, name="hsc", align_bytes=64)
+            nc.vector.quantize_mx(
+                out=hw[:].bitcast(FP8X4), scales=hsc[:], in_=hs[e][:].rearrange("p s t -> p (s t)")
+            )
+            if e % 4 == 0:
+                y_bank[e // 4] = psum_y.tile([N, 4, C], F32, name="yb")
+            yb = y_bank[e // 4]
+            nc.tensor.matmul_mx(
+                out=yb[:, e % 4, :],
+                lhsT=w2[:, e, :].bitcast(FP4X4),
+                lhsT_scale=w2s[:, e, :],
+                rhs=hw[:].bitcast(FP8X4),
+                rhs_scale=hsc[:],
+                start=True,
+                stop=True,
+            )
+            if e % 4 == 3:
+                nc.scalar.activation(
+                    y[:, (e - 3) * C : (e + 1) * C], yb[:].rearrange("n q s -> n (q s)"), ACT.Copy
+                )
+
+        starts = {}
+        e0 = 0
+        for n in GATHERS:
+            starts[max(0, e0 - 1)] = starts.get(max(0, e0 - 1), []) + [(e0, n)]
+            e0 += n
+        for step in range(E + 2):
+            for e0, n in starts.get(step, []):
+                gather(e0, n)
+            if step >= 2:
+                second(step - 2)
+            if 1 <= step <= E:
+                turn(step - 1)
+            if step < E:
+                first(step)
+
+        prods = {}
+
+        def product(i, r):
+            t0, t1 = OUT_CUTS[i], OUT_CUTS[i + 1]
+            pr = ring2.tile([P, t1 - t0], F32, name=f"pr{r}")
+            nc.vector.tensor_tensor(
+                pr[:], y[:].indirect(pos_sb[r][:, t0 // 16 : t1 // 16]), gate_sb[:, r, t0:t1], ALU.mult
+            )
+            prods[i, r] = pr
+
+        def add01(i):
+            s = ring2.tile([P, OUT_CUTS[i + 1] - OUT_CUTS[i]], F32, name="s01")
+            nc.vector.tensor_tensor(s[:], prods[i, 0][:], prods[i, 1][:], ALU.add)
+            prods[i, 3] = s
+
+        def add2(i):
+            t0, t1 = OUT_CUTS[i], OUT_CUTS[i + 1]
+            s = ring2.tile([P, t1 - t0], F32, name="s012")
+            nc.vector.tensor_tensor(s[:], prods[i, 3][:], prods[i, 2][:], ALU.add)
+            nc.sync.dma_start(out[:, t0:t1], s[:])
+
+        cuts = len(OUT_CUTS) - 1
+        for i in range(cuts):
+            product(i, 0)
+            product(i, 1)
+            if i > 0:
+                add2(i - 1)
+            product(i, 2)
+            add01(i)
+        add2(cuts - 1)

@@ -24,8 +24,6 @@ PACK = 4
 
 X_CUTS = [0, 256, 512, 768, 896, 1024]
 X_ON_SCALAR = (0, 2)
-GATHERS = [1, 1] + [2] * 11
-RELU_ON_VECTOR = (5, 7, 9, 11, 13, 15, 17, 19, 21, 23)
 OUT_CUTS = [0, 512, 768, 1024]
 
 
@@ -35,7 +33,7 @@ def tile_moe_tk_mlp_relu2_kernel(
     nc = tc.nc
     with ExitStack() as ctx:
         held = ctx.enter_context(tc.tile_pool(name="held", bufs=1))
-        ring = ctx.enter_context(tc.tile_pool(name="ring", bufs=4))
+        ring = ctx.enter_context(tc.tile_pool(name="ring", bufs=6))
         ring2 = ctx.enter_context(tc.tile_pool(name="ring2", bufs=2))
         psum_a = ctx.enter_context(tc.psum_pool(name="psum_a", bufs=3))
         psum_b = ctx.enter_context(tc.psum_pool(name="psum_b", bufs=3))
@@ -88,14 +86,17 @@ def tile_moe_tk_mlp_relu2_kernel(
 
         load_w1(0, 2)
         load_scales(w1s, w1_scales, 0, 6)
-        load_scales(w2s, w2_scales, 0, E)
-        load_w1(2, 5)
-        load_w2(0, 8)
-        load_scales(w1s, w1_scales, 6, E)
-        load_w1(5, 9)
-        load_w1(9, 14)
-        load_w2(8, E)
+        load_scales(w2s, w2_scales, 0, 6)
+        load_w1(2, 6)
+        load_w2(0, 6)
+        load_scales(w1s, w1_scales, 6, 14)
+        load_w1(6, 10)
+        load_scales(w2s, w2_scales, 6, E)
+        load_w1(10, 14)
+        load_w2(6, 14)
+        load_scales(w1s, w1_scales, 14, E)
         load_w1(14, 19)
+        load_w2(14, E)
         load_w1(19, E)
         for r, p in enumerate((pos1, pos2, pos3)):
             nc.sync.dma_start(pos_sb[r][:], p)
@@ -145,7 +146,7 @@ def tile_moe_tk_mlp_relu2_kernel(
             )
             r = ring.tile([C, PACK, P], F32, name="r")
             src = a[:].rearrange("s (m t) -> s t m", t=PACK)
-            if e in RELU_ON_VECTOR:
+            if e % 2 == 1:
                 nc.vector.tensor_scalar_max(r[:], src, 0.0)
             else:
                 nc.scalar.activation(r[:], src, ACT.Relu)
@@ -177,25 +178,28 @@ def tile_moe_tk_mlp_relu2_kernel(
                 start=True,
                 stop=True,
             )
-            if e % 4 == 3:
+            if e % 4 == 3 or e == E - 3:
+                lo = e - 1 if e >= E - 3 else e - 3
                 nc.scalar.activation(
-                    y[:, (e - 3) * C : (e + 1) * C], yb[:].rearrange("n q s -> n (q s)"), ACT.Copy
+                    y[:, lo * C : (e + 1) * C],
+                    yb[:, lo % 4 : e % 4 + 1, :].rearrange("n q s -> n (q s)"),
+                    ACT.Copy,
                 )
 
-        starts = {}
-        e0 = 0
-        for n in GATHERS:
-            starts[max(0, e0 - 1)] = starts.get(max(0, e0 - 1), []) + [(e0, n)]
-            e0 += n
-        for step in range(E + 2):
-            for e0, n in starts.get(step, []):
-                gather(e0, n)
-            if step >= 2:
-                second(step - 2)
-            if 1 <= step <= E:
-                turn(step - 1)
-            if step < E:
-                first(step)
+        gather(0, 2)
+        gather(2, 2)
+        for step in range(E // 2 + 3):
+            if step >= 3:
+                second(2 * step - 6)
+                second(2 * step - 5)
+            if 1 <= step <= E // 2:
+                turn(2 * step - 2)
+                turn(2 * step - 1)
+            if step < E // 2:
+                first(2 * step)
+                first(2 * step + 1)
+            if step + 2 < E // 2:
+                gather(2 * step + 4, 2)
 
         prods = {}
 

@@ -22,8 +22,10 @@ ALU = mybir.AluOpType
 P = 128
 PACK = 4
 
-X_CUTS = [0, 256, 512, 768, 896, 1024]
-X_ON_SCALAR = (0, 2)
+X_LOADS = [0, 512, 768, 1024]
+X_CUTS = [0, 256, 512, 640, 768, 896, 1024]
+X_ON_SCALAR = (0, 2, 4)
+RELU_ON_VECTOR = (3, 5, 7, 9, 10, 11, 13, 15, 17, 19, 20, 21, 22, 23)
 OUT_CUTS = [0, 512, 768, 1024]
 
 
@@ -53,19 +55,17 @@ def tile_moe_tk_mlp_relu2_kernel(
 
         nc.gpsimd.memset(x_scales[:], 0)
         make_identity(nc, ident[:])
-        nc.vector.memset(w1s[:, 0:6, :].bitcast(I32), 0)
-        nc.vector.memset(w2s[:].bitcast(I32), 0)
-        nc.vector.memset(w1s[:, 6:E, :].bitcast(I32), 0)
+        nc.vector.memset(w1s[:, 0:8, :].bitcast(I32), 0)
+        nc.vector.memset(w2s[:, 0:8, :].bitcast(I32), 0)
+        nc.gpsimd.memset(w1s[:, 8:E, :].bitcast(I32), 0)
+        nc.gpsimd.memset(w2s[:, 8:E, :].bitcast(I32), 0)
 
-        x_raw = []
+        x_raw = held.tile([P, PACK, T], F32, name="x_raw")
         x_view = xT.rearrange("(p j) t -> p j t", j=PACK)
-        for i in range(len(X_CUTS) - 1):
-            t0, t1 = X_CUTS[i], X_CUTS[i + 1]
-            raw = held.tile([P, PACK, t1 - t0], F32, name=f"x_raw{i}")
-            nc.sync.dma_start(raw[:], x_view[:, :, t0:t1])
-            x_raw.append(raw)
-            if i == len(X_CUTS) - 3:
-                nc.sync.dma_start(offs_sb[:], offs)
+
+        def load_x(i):
+            cols = slice(X_LOADS[i], X_LOADS[i + 1])
+            nc.sync.dma_start(x_raw[:, :, cols], x_view[:, :, cols])
 
         def load_w1(a, b):
             nc.sync.dma_start(
@@ -77,27 +77,29 @@ def tile_moe_tk_mlp_relu2_kernel(
                 w2[:, a:b, :].bitcast(I32), w2_words[a:b, 0].rearrange("e p n -> p e n").bitcast(I32)
             )
 
-        def load_scales(tile, src, a, b):
+        def load_scales(queue, tile, src, a, b):
             for q in range(4):
-                nc.sync.dma_start(
+                queue.dma_start(
                     tile[32 * q : 32 * q + 4, a:b, :].bitcast(I32),
                     src[a:b, 0, 4 * q : 4 * q + 4, :].rearrange("e q n -> q e n").bitcast(I32),
                 )
 
+        load_scales(nc.gpsimd, w1s, w1_scales, 8, E)
+        load_scales(nc.gpsimd, w2s, w2_scales, 8, E)
+        load_x(0)
+        load_x(1)
+        load_scales(nc.sync, w1s, w1_scales, 0, 8)
+        nc.sync.dma_start(offs_sb[:], offs)
+        load_x(2)
         load_w1(0, 2)
-        load_scales(w1s, w1_scales, 0, 6)
-        load_scales(w2s, w2_scales, 0, 6)
+        load_scales(nc.sync, w2s, w2_scales, 0, 8)
         load_w1(2, 6)
         load_w2(0, 6)
-        load_scales(w1s, w1_scales, 6, 14)
-        load_w1(6, 10)
-        load_scales(w2s, w2_scales, 6, E)
-        load_w1(10, 14)
+        load_w1(6, 12)
         load_w2(6, 14)
-        load_scales(w1s, w1_scales, 14, E)
-        load_w1(14, 19)
+        load_w1(12, 18)
         load_w2(14, E)
-        load_w1(19, E)
+        load_w1(18, E)
         for r, p in enumerate((pos1, pos2, pos3)):
             nc.sync.dma_start(pos_sb[r][:], p)
         nc.sync.dma_start(gate_sb[:], gate.rearrange("r p t -> p r t"))
@@ -105,7 +107,7 @@ def tile_moe_tk_mlp_relu2_kernel(
         for i in range(len(X_CUTS) - 1):
             t0, t1 = X_CUTS[i], X_CUTS[i + 1]
             grouped = held.tile([P, t1 - t0, PACK], BF16, name=f"x_grouped{i}", align_bytes=64)
-            src = x_raw[i][:].rearrange("p j t -> p t j")
+            src = x_raw[:, :, t0:t1].rearrange("p j t -> p t j")
             if i in X_ON_SCALAR:
                 nc.scalar.activation(grouped[:], src, ACT.Copy)
             else:
@@ -116,7 +118,7 @@ def tile_moe_tk_mlp_relu2_kernel(
                 in_=grouped[:].rearrange("p t j -> p (t j)"),
             )
 
-        gath = ctx.enter_context(tc.tile_pool(name="gath", bufs=3))
+        gath = ctx.enter_context(tc.tile_pool(name="gath", bufs=4))
         gathered = {}
 
         def gather(e0, n):
@@ -146,7 +148,7 @@ def tile_moe_tk_mlp_relu2_kernel(
             )
             r = ring.tile([C, PACK, P], F32, name="r")
             src = a[:].rearrange("s (m t) -> s t m", t=PACK)
-            if e % 2 == 1:
+            if e in RELU_ON_VECTOR:
                 nc.vector.tensor_scalar_max(r[:], src, 0.0)
             else:
                 nc.scalar.activation(r[:], src, ACT.Relu)

from contextlib import ExitStack

import concourse.mybir as mybir
from concourse.masks import make_identity

K, T, E, C, H, N = 512, 1024, 24, 128, 512, 128
TOP = 3
S = E * C
FLOPS = 2 * S * (K * H + H * N)

F32 = mybir.dt.float32
BF16 = mybir.dt.bfloat16
I32 = mybir.dt.int32
U32 = mybir.dt.uint32
U16 = mybir.dt.uint16
U8 = mybir.dt.uint8
FP8X4 = mybir.dt.float8_e4m3fn_x4
FP4X4 = mybir.dt.float4_e2m1fn_x4
ACT = mybir.ActivationFunctionType
ALU = mybir.AluOpType

P = 128
PACK = 4

X_LOADS = [0, 512, 768, 1024]
X_CUTS = [0, 256, 512, 640, 768, 896, 1024]
X_ON_SCALAR = (0, 2, 4)
RELU_ON_VECTOR = (3, 5, 7, 9, 10, 11, 13, 15, 17, 19, 20, 21, 22, 23)
OUT_CUTS = [0, 512, 768, 1024]


def tile_moe_tk_mlp_relu2_kernel(
    tc, xT, w1_words, w1_scales, w2_words, w2_scales, gate, offs, pos1, pos2, pos3, out
):
    nc = tc.nc
    with ExitStack() as ctx:
        held = ctx.enter_context(tc.tile_pool(name="held", bufs=1))
        ring = ctx.enter_context(tc.tile_pool(name="ring", bufs=6))
        ring2 = ctx.enter_context(tc.tile_pool(name="ring2", bufs=2))
        psum_a = ctx.enter_context(tc.psum_pool(name="psum_a", bufs=3))
        psum_b = ctx.enter_context(tc.psum_pool(name="psum_b", bufs=3))
        psum_y = ctx.enter_context(tc.psum_pool(name="psum_y", bufs=2))

        offs_sb = held.tile([P, S // 16], U16, name="offs_sb")
        pos_sb = [held.tile([P, T // 16], U16, name=f"pos{r}_sb") for r in range(TOP)]
        x_words = held.tile([P, T], U32, name="x_words", align_bytes=64)
        x_scales = held.tile([P, T], U8, name="x_scales", align_bytes=64)
        w1 = held.tile([P, E, 2 * H], U8, name="w1", align_bytes=64)
        w1s = held.tile([P, E, H], U8, name="w1s", align_bytes=64)
        w2 = held.tile([P, E, 2 * N], U8, name="w2", align_bytes=64)
        w2s = held.tile([P, E, N], U8, name="w2s", align_bytes=64)
        gate_sb = held.tile([P, TOP, T], F32, name="gate_sb")
        y = held.tile([P, S], F32, name="y")
        ident = held.tile([P, P], F32, name="ident")

        nc.gpsimd.memset(x_scales[:], 0)
        make_identity(nc, ident[:])
        nc.vector.memset(w1s[:, 0:8, :].bitcast(I32), 0)
        nc.vector.memset(w2s[:, 0:8, :].bitcast(I32), 0)
        nc.gpsimd.memset(w1s[:, 8:E, :].bitcast(I32), 0)
        nc.gpsimd.memset(w2s[:, 8:E, :].bitcast(I32), 0)

        x_raw = held.tile([P, PACK, T], F32, name="x_raw")
        x_view = xT.rearrange("(p j) t -> p j t", j=PACK)

        def load_x(i):
            cols = slice(X_LOADS[i], X_LOADS[i + 1])
            nc.sync.dma_start(x_raw[:, :, cols], x_view[:, :, cols])

        def load_w1(a, b):
            nc.sync.dma_start(
                w1[:, a:b, :].bitcast(I32), w1_words[a:b, 0].rearrange("e p n -> p e n").bitcast(I32)
            )

        def load_w2(a, b):
            nc.sync.dma_start(
                w2[:, a:b, :].bitcast(I32), w2_words[a:b, 0].rearrange("e p n -> p e n").bitcast(I32)
            )

        def load_scales(queue, tile, src, a, b):
            for q in range(4):
                queue.dma_start(
                    tile[32 * q : 32 * q + 4, a:b, :].bitcast(I32),
                    src[a:b, 0, 4 * q : 4 * q + 4, :].rearrange("e q n -> q e n").bitcast(I32),
                )

        load_scales(nc.gpsimd, w1s, w1_scales, 8, E)
        load_scales(nc.gpsimd, w2s, w2_scales, 8, E)
        load_x(0)
        load_x(1)
        load_scales(nc.sync, w1s, w1_scales, 0, 8)
        nc.sync.dma_start(offs_sb[:], offs)
        load_x(2)
        load_w1(0, 2)
        load_scales(nc.sync, w2s, w2_scales, 0, 8)
        load_w1(2, 6)
        load_w2(0, 6)
        load_w1(6, 12)
        load_w2(6, 14)
        load_w1(12, 18)
        load_w2(14, E)
        load_w1(18, E)
        for r, p in enumerate((pos1, pos2, pos3)):
            nc.sync.dma_start(pos_sb[r][:], p)
        nc.sync.dma_start(gate_sb[:], gate.rearrange("r p t -> p r t"))

        for i in range(len(X_CUTS) - 1):
            t0, t1 = X_CUTS[i], X_CUTS[i + 1]
            grouped = held.tile([P, t1 - t0, PACK], BF16, name=f"x_grouped{i}", align_bytes=64)
            src = x_raw[:, :, t0:t1].rearrange("p j t -> p t j")
            if i in X_ON_SCALAR:
                nc.scalar.activation(grouped[:], src, ACT.Copy)
            else:
                nc.vector.tensor_copy(grouped[:], src)
            nc.vector.quantize_mx(
                out=x_words[:, t0:t1].bitcast(FP8X4),
                scales=x_scales[:, t0:t1],
                in_=grouped[:].rearrange("p t j -> p (t j)"),
            )

        gath = ctx.enter_context(tc.tile_pool(name="gath", bufs=4))
        gathered = {}

        def gather(e0, n):
            cols = slice(e0 * C // 16, (e0 + n) * C // 16)
            gw = gath.tile([P, n * C], U32, name="gw", align_bytes=64)
            gs = gath.tile([P, n * C], U8, name="gs", align_bytes=64)
            nc.vector.tensor_copy(gw[:], x_words[:].indirect(offs_sb[:, cols]))
            nc.vector.tensor_copy(gs[:], x_scales[:].indirect(offs_sb[:, cols]))
            for e in range(e0, e0 + n):
                gathered[e] = (gw, gs, (e - e0) * C)

        acts = {}
        hs = {}
        y_bank = {}

        def first(e):
            gw, gs, c0 = gathered[e]
            a = psum_a.tile([C, H], F32, name="a")
            nc.tensor.matmul_mx(
                out=a[:],
                lhsT=gw[:, c0 : c0 + C].bitcast(FP8X4),
                lhsT_scale=gs[:, c0 : c0 + C],
                rhs=w1[:, e, :].bitcast(FP4X4),
                rhs_scale=w1s[:, e, :],
                start=True,
                stop=True,
            )
            r = ring.tile([C, PACK, P], F32, name="r")
            src = a[:].rearrange("s (m t) -> s t m", t=PACK)
            if e in RELU_ON_VECTOR:
                nc.vector.tensor_scalar_max(r[:], src, 0.0)
            else:
                nc.scalar.activation(r[:], src, ACT.Relu)
            acts[e] = r

        def turn(e):
            b = psum_b.tile([P, PACK, C], F32, name="b")
            for t in range(PACK):
                nc.tensor.transpose(b[:, t, :], acts[e][:, t, :], ident[:])
            h = ring.tile([P, C, PACK], BF16, name="h", align_bytes=64)
            nc.scalar.activation(h[:], b[:].rearrange("p t s -> p s t"), ACT.Square)
            hs[e] = h

        def second(e):
            hw = ring.tile([P, C], U32, name="hw", align_bytes=64)
            hsc = ring.tile([P, C], U8, name="hsc", align_bytes=64)
            nc.vector.quantize_mx(
                out=hw[:].bitcast(FP8X4), scales=hsc[:], in_=hs[e][:].rearrange("p s t -> p (s t)")
            )
            if e % 4 == 0:
                y_bank[e // 4] = psum_y.tile([N, 4, C], F32, name="yb")
            yb = y_bank[e // 4]
            nc.tensor.matmul_mx(
                out=yb[:, e % 4, :],
                lhsT=w2[:, e, :].bitcast(FP4X4),
                lhsT_scale=w2s[:, e, :],
                rhs=hw[:].bitcast(FP8X4),
                rhs_scale=hsc[:],
                start=True,
                stop=True,
            )
            if e % 4 == 3 or e == E - 3:
                lo = e - 1 if e >= E - 3 else e - 3
                nc.scalar.activation(
                    y[:, lo * C : (e + 1) * C],
                    yb[:, lo % 4 : e % 4 + 1, :].rearrange("n q s -> n (q s)"),
                    ACT.Copy,
                )

        gather(0, 2)
        gather(2, 2)
        for step in range(E // 2 + 3):
            if step >= 3:
                second(2 * step - 6)
                second(2 * step - 5)
            if 1 <= step <= E // 2:
                turn(2 * step - 2)
                turn(2 * step - 1)
            if step < E // 2:
                first(2 * step)
                first(2 * step + 1)
            if step + 2 < E // 2:
                gather(2 * step + 4, 2)

        prods = {}

        def product(i, r):
            t0, t1 = OUT_CUTS[i], OUT_CUTS[i + 1]
            pr = ring2.tile([P, t1 - t0], F32, name=f"pr{r}")
            nc.vector.tensor_tensor(
                pr[:], y[:].indirect(pos_sb[r][:, t0 // 16 : t1 // 16]), gate_sb[:, r, t0:t1], ALU.mult
            )
            prods[i, r] = pr

        def add01(i):
            s = ring2.tile([P, OUT_CUTS[i + 1] - OUT_CUTS[i]], F32, name="s01")
            nc.vector.tensor_tensor(s[:], prods[i, 0][:], prods[i, 1][:], ALU.add)
            prods[i, 3] = s

        def add2(i):
            t0, t1 = OUT_CUTS[i], OUT_CUTS[i + 1]
            s = ring2.tile([P, t1 - t0], F32, name="s012")
            nc.vector.tensor_tensor(s[:], prods[i, 3][:], prods[i, 2][:], ALU.add)
            nc.sync.dma_start(out[:, t0:t1], s[:])

        cuts = len(OUT_CUTS) - 1
        for i in range(cuts):
            product(i, 0)
            product(i, 1)
            if i > 0:
                add2(i - 1)
            product(i, 2)
            add01(i)
        add2(cuts - 1)
